import numpy as np, ml_dtypes
CORES = [56,61,80,85]
N = 4
QP = 64
def setup_inputs(rng):
    return {"q": rng.standard_normal((N, 128, QP), dtype=np.float32).astype(ml_dtypes.bfloat16), "k": rng.standard_normal((N, 128, 128), dtype=np.float32).astype(ml_dtypes.bfloat16), "v": rng.standard_normal((N, 128, 128), dtype=np.float32).astype(ml_dtypes.bfloat16), "b": (8 * rng.standard_normal((N, 128, N * QP), dtype=np.float32)).astype(ml_dtypes.bfloat16)}
def setup_inputs_big(rng):
    d = setup_inputs(rng)
    for k in ("q", "k", "v", "b"): d[k] = (d[k].astype(np.float32) * 1024.0).astype(d[k].dtype)
    return d
def setup_inputs_small(rng):
    d = setup_inputs(rng)
    for k in ("q", "k", "v", "b"): d[k] = (d[k].astype(np.float32) * (1 / 1024.0)).astype(d[k].dtype)
    return d
def setup_inputs_apart(rng):
    d = setup_inputs(rng)
    f = (10.0 ** rng.permutation(np.linspace(-1.5, 1.5, N))).astype(np.float32).reshape(N, 1, 1)
    for k in ("q", "k", "v", "b"): d[k] = (d[k].astype(np.float32) * f).astype(d[k].dtype)
    return d
def reference(q, k, v, b):
    Q, K, V, B = q.astype(np.float64), k.astype(np.float64), v.astype(np.float64), b.astype(np.float64)
    y = np.zeros((N, 128, QP))
    for r in range(N):
        for j in range(N):
            y[r] += V[j].T @ np.maximum(K[j].T @ Q[r] + B[r][:, QP * j:QP * j + QP], 0.0)
    return {"y": y.astype(ml_dtypes.bfloat16 if q.dtype != np.float64 else np.float64)}

@@ -1,0 +1,155 @@
+from concourse.bass import DstId, RemoteDMATransfer
+from concourse.mybir import AluOpType
+
+NSIM = 96
+N = 4
+QP = 64
+KP = 128
+FT = 128
+W = KP + FT
+
+SCRATCH = {
+    "stage": ("dram", [128, W], "bfloat16"),
+    "kv": ("sbuf", [128, N * W], "bfloat16"),
+    "qs": ("sbuf", [128, QP], "bfloat16"),
+    "bs": ("sbuf", [128, N * QP], "bfloat16"),
+    "zero": ("sbuf", [128, 2 * QP], "bfloat16"),
+    "s_near": ("sbuf", [128, 2 * QP], "bfloat16"),
+    "s_far": ("sbuf", [128, 2 * QP], "bfloat16"),
+    "ysb": ("sbuf", [128, QP], "bfloat16"),
+    "p_near": ("psum", [128, 512], "float32"),
+    "t_near": ("psum", [128, 512], "float32"),
+    "p_far": ("psum", [128, 512], "float32"),
+    "t_far": ("psum", [128, 512], "float32"),
+    "p_out": ("psum", [128, 512], "float32"),
+}
+SEMAPHORES = ["ld", "ldqb", "own", "arr", "far", "peer", "sent", "sent2", "zs",
+              "mm_near", "va_near", "vs_near", "mm_far", "va_far", "vs_far", "mo", "vy", "st"]
+
+
+def _bits(mask):
+    return [i for i in range(mask.bit_length()) if (mask >> i) & 1]
+
+
+def _mask_of(bits):
+    m = 0
+    for i in bits:
+        m |= 1 << i
+    return m
+
+
+def _relays(cores, topo):
+    out = {}
+    for r, c in enumerate(cores):
+        far = [j for j, d in enumerate(cores) if topo.chip(d) != topo.chip(c)]
+        helpers = [h for h in range(NSIM)
+                   if topo.chip(h) == topo.chip(c) and topo.die(h) == topo.die(c) and h not in cores
+                   and all(topo.may_write(h, cores[j]) for j in far)]
+        for i, j in enumerate(far):
+            out[(r, j)] = helpers[i]
+    return out
+
+
+def _split_masks(core, helpers, topo):
+    full = topo.mask(core, helpers[0])
+    for h in helpers[1:]:
+        full &= topo.mask(core, h)
+    bits = _bits(full)
+    n = len(bits) // len(helpers)
+    return [_mask_of(bits[i * n:(i + 1) * n]) for i in range(len(helpers))]
+
+
+def _pair(g, T, js, p, t, sbuf, mm, va, vs, first, last, done):
+    lo, hi = js[0] * QP, (js[-1] + 1) * QP
+    n = hi - lo
+    for i, j in enumerate(js):
+        g.tensor.matmul(out=p[:, i * QP:(i + 1) * QP], lhsT=T.kv[:, j * W:j * W + KP], rhs=T.qs[:],
+                        start=True, stop=True).then_inc(mm, 1)
+    g.vector.wait_ge(mm, len(js))
+    g.vector.tensor_tensor(out=t[:, 0:n], in0=p[:, 0:n], in1=T.bs[:, lo:hi], op=AluOpType.add).then_inc(va, 1)
+    g.vector.wait_ge(va, 1)
+    g.vector.tensor_tensor(out=sbuf[:, 0:n], in0=t[:, 0:n], in1=T.zero[:, 0:n], op=AluOpType.max).then_inc(vs, 1)
+    g.tensor.wait_ge(vs, 1)
+    for i, j in enumerate(js):
+        ins = g.tensor.matmul(out=T.p_out[:, 0:QP], lhsT=T.kv[:, j * W + KP:(j + 1) * W],
+                              rhs=sbuf[:, i * QP:(i + 1) * QP],
+                              start=(first and i == 0), stop=(last and i == len(js) - 1))
+        if last and i == len(js) - 1:
+            ins.then_inc(done, 1)
+
+
+def rank_program(g, core, T, topo):
+    cores = list(T.cores)
+    relay_of = _relays(cores, topo)
+    s = T.sem
+    rank = T.rank_of(core)
+
+    if rank is None:
+        jobs = [rj for rj, h in relay_of.items() if h == core]
+        if not jobs:
+            return
+        r, j = jobs[0]
+        src = cores[r]
+        mine = [relay_of[(r, x)] for x in range(N) if (r, x) in relay_of]
+        n_in = len(_bits(_split_masks(src, mine, topo)[mine.index(core)]))
+        dst = cores[j]
+        rid, pid, _se = topo.addr(dst)
+        m = topo.mask(core, dst)
+        g.wait_ge(s.arr, n_in)
+        g.remote_dma(out_ap=T.kv[:, r * W:(r + 1) * W], in_ap=T.stage[:], remote_sem=s.far, local_sem=s.sent,
+                     pid=pid, routing_id=rid, dma_engine_mask=m)
+        g.wait_ge(s.sent, len(_bits(m)))
+        return
+
+    near = [j for j, d in enumerate(cores) if topo.chip(d) == topo.chip(core)]
+    far = [j for j, d in enumerate(cores) if topo.chip(d) != topo.chip(core)]
+    peers = [j for j in near if j != rank]
+    helpers = [relay_of[(rank, j)] for j in far]
+    masks = _split_masks(core, helpers, topo)
+
+    g.sync.dma_start(T.stage[:, 0:KP], T.k[:]).then_inc(s.ld, 16)
+    g.scalar.dma_start(T.stage[:, KP:W], T.v[:]).then_inc(s.ld, 16)
+    g.sync.dma_start(T.qs[:], T.q[:]).then_inc(s.ldqb, 16)
+    g.scalar.dma_start(T.bs[:], T.b[:]).then_inc(s.ldqb, 16)
+    g.vector.memset(T.zero[:], 0.0).then_inc(s.zs, 1)
+
+    g.wait_ge(s.ld, 32)
+    trs = []
+    for h, m in zip(helpers, masks):
+        rid, pid, _se = topo.addr(h)
+        trs.append(RemoteDMATransfer(dst_ids=[DstId(rid=rid, pnc=pid)], dma_engine_mask=m, remote_sem=s.arr,
+                                     src=T.stage[:], dst=T.stage[:]))
+    g.remote_dma_fused(trs, local_sem=s.sent)
+    n_sent = sum(len(_bits(m)) for m in masks)
+
+    n_sent2 = 0
+    for j in peers:
+        rid, pid, _se = topo.addr(cores[j])
+        m = topo.mask(core, cores[j])
+        g.remote_dma(out_ap=T.kv[:, rank * W:(rank + 1) * W], in_ap=T.stage[:], remote_sem=s.peer,
+                     local_sem=s.sent2, pid=pid, routing_id=rid, dma_engine_mask=m)
+        n_sent2 += len(_bits(m))
+
+    g.sync.wait_ge(s.ld, 32)
+    g.sync.wait_ge(s.sent, n_sent)
+    g.sync.dma_start(T.kv[:, rank * W:(rank + 1) * W], T.stage[:]).then_inc(s.own, 16)
+
+    g.vector.wait_ge(s.zs, 1)
+    g.vector.wait_ge(s.ldqb, 32)
+    g.tensor.wait_ge(s.ldqb, 32)
+    g.tensor.wait_ge(s.own, 16)
+    n_peer = sum(len(_bits(topo.mask(cores[j], core))) for j in peers)
+    g.tensor.wait_ge(s.peer, n_peer)
+    _pair(g, T, near, T.p_near, T.t_near, T.s_near, s.mm_near, s.va_near, s.vs_near, True, False, s.mo)
+    n_far = sum(len(_bits(topo.mask(relay_of[(j, rank)], core))) for j in far)
+    g.tensor.wait_ge(s.far, n_far)
+    _pair(g, T, far, T.p_far, T.t_far, T.s_far, s.mm_far, s.va_far, s.vs_far, False, True, s.mo)
+
+    g.vector.wait_ge(s.mo, 1)
+    g.vector.tensor_copy(out=T.ysb[:], in_=T.p_out[:, 0:QP]).then_inc(s.vy, 1)
+    g.sync.wait_ge(s.vy, 1)
+    g.sync.dma_start(T.y[:], T.ysb[:]).then_inc(s.st, 16)
+    g.sync.wait_ge(s.st, 16)
+
+    g.wait_ge(s.sent, n_sent)
+    g.wait_ge(s.sent2, n_sent2)

@@ -13,18 +13,18 @@ SCRATCH = {
     "kv": ("sbuf", [128, N * W], "bfloat16"),
     "qs": ("sbuf", [128, QP], "bfloat16"),
     "bs": ("sbuf", [128, N * QP], "bfloat16"),
-    "zero": ("sbuf", [128, 2 * QP], "bfloat16"),
-    "s_near": ("sbuf", [128, 2 * QP], "bfloat16"),
-    "s_far": ("sbuf", [128, 2 * QP], "bfloat16"),
+    "nb": ("sbuf", [128, N * QP], "bfloat16"),
+    "zero": ("sbuf", [128, N * QP], "bfloat16"),
+    "sm": ("sbuf", [128, N * QP], "bfloat16"),
     "ysb": ("sbuf", [128, QP], "bfloat16"),
-    "p_near": ("psum", [128, 512], "float32"),
-    "t_near": ("psum", [128, 512], "float32"),
-    "p_far": ("psum", [128, 512], "float32"),
-    "t_far": ("psum", [128, 512], "float32"),
+    "p0": ("psum", [128, 512], "float32"),
+    "p1": ("psum", [128, 512], "float32"),
+    "p2": ("psum", [128, 512], "float32"),
+    "p3": ("psum", [128, 512], "float32"),
     "p_out": ("psum", [128, 512], "float32"),
 }
-SEMAPHORES = ["ld", "ldqb", "own", "arr", "far", "peer", "sent", "sent2", "zs",
-              "mm_near", "va_near", "vs_near", "mm_far", "va_far", "vs_far", "mo", "vy", "st"]
+SEMAPHORES = (["ld", "ldqb", "own", "arr", "peer", "sent", "sent2", "zs", "nbs", "mo", "vy", "st"]
+              + ["far%d" % j for j in range(N)] + ["mm%d" % j for j in range(N)] + ["vs%d" % j for j in range(N)])
 
 
 def _bits(mask):
@@ -59,23 +59,26 @@ def _split_masks(core, helpers, topo):
     return [_mask_of(bits[i * n:(i + 1) * n]) for i in range(len(helpers))]
 
 
-def _pair(g, T, js, p, t, sbuf, mm, va, vs, first, last, done):
-    lo, hi = js[0] * QP, (js[-1] + 1) * QP
-    n = hi - lo
+def _group(g, T, js, waits, first, last):
+    s = T.sem
+    for j in js:
+        for sem, cnt in waits[j]:
+            g.tensor.wait_ge(sem, cnt)
+        g.tensor.matmul(out=T["p%d" % j][:, 0:QP], lhsT=T.kv[:, j * W:j * W + KP], rhs=T.qs[:],
+                        start=True, stop=True).then_inc(s["mm%d" % j], 1)
+        g.vector.wait_ge(s["mm%d" % j], 1)
+        g.vector.tensor_tensor(out=T.sm[:, j * QP:(j + 1) * QP], in0=T["p%d" % j][:, 0:QP],
+                               in1=T.nb[:, j * QP:(j + 1) * QP], op=AluOpType.max).then_inc(s["vs%d" % j], 1)
     for i, j in enumerate(js):
-        g.tensor.matmul(out=p[:, i * QP:(i + 1) * QP], lhsT=T.kv[:, j * W:j * W + KP], rhs=T.qs[:],
-                        start=True, stop=True).then_inc(mm, 1)
-    g.vector.wait_ge(mm, len(js))
-    g.vector.tensor_tensor(out=t[:, 0:n], in0=p[:, 0:n], in1=T.bs[:, lo:hi], op=AluOpType.add).then_inc(va, 1)
-    g.vector.wait_ge(va, 1)
-    g.vector.tensor_tensor(out=sbuf[:, 0:n], in0=t[:, 0:n], in1=T.zero[:, 0:n], op=AluOpType.max).then_inc(vs, 1)
-    g.tensor.wait_ge(vs, 1)
+        g.tensor.matmul(out=T.p_out[:, 0:QP], lhsT=T.kv[:, j * W + KP:(j + 1) * W], rhs=T.bs[:, j * QP:(j + 1) * QP],
+                        start=(first and i == 0), stop=False)
     for i, j in enumerate(js):
+        g.tensor.wait_ge(s["vs%d" % j], 1)
+        end = last and i == len(js) - 1
         ins = g.tensor.matmul(out=T.p_out[:, 0:QP], lhsT=T.kv[:, j * W + KP:(j + 1) * W],
-                              rhs=sbuf[:, i * QP:(i + 1) * QP],
-                              start=(first and i == 0), stop=(last and i == len(js) - 1))
-        if last and i == len(js) - 1:
-            ins.then_inc(done, 1)
+                              rhs=T.sm[:, j * QP:(j + 1) * QP], start=False, stop=end)
+        if end:
+            ins.then_inc(s.mo, 1)
 
 
 def rank_program(g, core, T, topo):
@@ -96,8 +99,8 @@ def rank_program(g, core, T, topo):
         rid, pid, _se = topo.addr(dst)
         m = topo.mask(core, dst)
         g.wait_ge(s.arr, n_in)
-        g.remote_dma(out_ap=T.kv[:, r * W:(r + 1) * W], in_ap=T.stage[:], remote_sem=s.far, local_sem=s.sent,
-                     pid=pid, routing_id=rid, dma_engine_mask=m)
+        g.remote_dma(out_ap=T.kv[:, r * W:(r + 1) * W], in_ap=T.stage[:], remote_sem=s["far%d" % r],
+                     local_sem=s.sent, pid=pid, routing_id=rid, dma_engine_mask=m)
         g.wait_ge(s.sent, len(_bits(m)))
         return
 
@@ -136,14 +139,18 @@ def rank_program(g, core, T, topo):
 
     g.vector.wait_ge(s.zs, 1)
     g.vector.wait_ge(s.ldqb, 32)
-    g.tensor.wait_ge(s.ldqb, 32)
-    g.tensor.wait_ge(s.own, 16)
+    g.vector.tensor_tensor(out=T.nb[:], in0=T.zero[:], in1=T.bs[:], op=AluOpType.subtract).then_inc(s.nbs, 1)
+    g.vector.wait_ge(s.nbs, 1)
+
     n_peer = sum(len(_bits(topo.mask(cores[j], core))) for j in peers)
-    g.tensor.wait_ge(s.peer, n_peer)
-    _pair(g, T, near, T.p_near, T.t_near, T.s_near, s.mm_near, s.va_near, s.vs_near, True, False, s.mo)
-    n_far = sum(len(_bits(topo.mask(relay_of[(j, rank)], core))) for j in far)
-    g.tensor.wait_ge(s.far, n_far)
-    _pair(g, T, far, T.p_far, T.t_far, T.s_far, s.mm_far, s.va_far, s.vs_far, False, True, s.mo)
+    waits = {rank: [(s.own, 16)]}
+    for j in peers:
+        waits[j] = [(s.peer, n_peer)]
+    for j in far:
+        waits[j] = [(s["far%d" % j], len(_bits(topo.mask(relay_of[(j, rank)], core))))]
+    g.tensor.wait_ge(s.ldqb, 32)
+    _group(g, T, [rank] + peers, waits, True, False)
+    _group(g, T, far, waits, False, True)
 
     g.vector.wait_ge(s.mo, 1)
     g.vector.tensor_copy(out=T.ysb[:], in_=T.p_out[:, 0:QP]).then_inc(s.vy, 1)

@@ -9,7 +9,8 @@ FT = 128
 W = KP + FT
 
 SCRATCH = {
-    "stage": ("dram", [128, W], "bfloat16"),
+    "dk": ("dram", [128, KP], "bfloat16"),
+    "dv": ("dram", [128, FT], "bfloat16"),
     "kv": ("sbuf", [128, N * W], "bfloat16"),
     "qs": ("sbuf", [128, QP], "bfloat16"),
     "bs": ("sbuf", [128, N * QP], "bfloat16"),
@@ -23,8 +24,9 @@ SCRATCH = {
     "p3": ("psum", [128, 512], "float32"),
     "p_out": ("psum", [128, 512], "float32"),
 }
-SEMAPHORES = (["ld", "ldqb", "own", "arr", "peer", "sent", "sent2", "zs", "nbs", "mo", "vy", "st"]
-              + ["far%d" % j for j in range(N)] + ["mm%d" % j for j in range(N)] + ["vs%d" % j for j in range(N)])
+SEMAPHORES = (["ldk", "ldv", "ldqb", "own", "arrk", "arrv", "peer", "sent", "zs", "nbs", "mo", "vy", "st"]
+              + ["fk%d" % j for j in range(N)] + ["fv%d" % j for j in range(N)]
+              + ["mm%d" % j for j in range(N)] + ["vs%d" % j for j in range(N)])
 
 
 def _bits(mask):
@@ -50,26 +52,26 @@ def _relays(cores, topo):
     return out
 
 
-def _split_masks(core, helpers, topo):
-    full = topo.mask(core, helpers[0])
-    for h in helpers[1:]:
+def _split_masks(core, dsts, topo):
+    full = topo.mask(core, dsts[0])
+    for h in dsts[1:]:
         full &= topo.mask(core, h)
     bits = _bits(full)
-    n = len(bits) // len(helpers)
-    return [_mask_of(bits[i * n:(i + 1) * n]) for i in range(len(helpers))]
+    n = len(bits) // len(dsts)
+    return [_mask_of(bits[i * n:(i + 1) * n]) for i in range(len(dsts))]
 
 
-def _group(g, T, js, waits, first, last):
+def _group(g, T, js, wk, wv, first, last):
     s = T.sem
     for j in js:
-        for sem, cnt in waits[j]:
-            g.tensor.wait_ge(sem, cnt)
+        g.tensor.wait_ge(wk[j][0], wk[j][1])
         g.tensor.matmul(out=T["p%d" % j][:, 0:QP], lhsT=T.kv[:, j * W:j * W + KP], rhs=T.qs[:],
                         start=True, stop=True).then_inc(s["mm%d" % j], 1)
         g.vector.wait_ge(s["mm%d" % j], 1)
         g.vector.tensor_tensor(out=T.sm[:, j * QP:(j + 1) * QP], in0=T["p%d" % j][:, 0:QP],
                                in1=T.nb[:, j * QP:(j + 1) * QP], op=AluOpType.max).then_inc(s["vs%d" % j], 1)
     for i, j in enumerate(js):
+        g.tensor.wait_ge(wv[j][0], wv[j][1])
         g.tensor.matmul(out=T.p_out[:, 0:QP], lhsT=T.kv[:, j * W + KP:(j + 1) * W], rhs=T.bs[:, j * QP:(j + 1) * QP],
                         start=(first and i == 0), stop=False)
     for i, j in enumerate(js):
@@ -92,16 +94,18 @@ def rank_program(g, core, T, topo):
         if not jobs:
             return
         r, j = jobs[0]
-        src = cores[r]
         mine = [relay_of[(r, x)] for x in range(N) if (r, x) in relay_of]
-        n_in = len(_bits(_split_masks(src, mine, topo)[mine.index(core)]))
+        n_in = len(_bits(_split_masks(cores[r], mine, topo)[mine.index(core)]))
         dst = cores[j]
         rid, pid, _se = topo.addr(dst)
         m = topo.mask(core, dst)
-        g.wait_ge(s.arr, n_in)
-        g.remote_dma(out_ap=T.kv[:, r * W:(r + 1) * W], in_ap=T.stage[:], remote_sem=s["far%d" % r],
+        g.wait_ge(s.arrk, n_in)
+        g.remote_dma(out_ap=T.kv[:, r * W:r * W + KP], in_ap=T.dk[:], remote_sem=s["fk%d" % r],
                      local_sem=s.sent, pid=pid, routing_id=rid, dma_engine_mask=m)
-        g.wait_ge(s.sent, len(_bits(m)))
+        g.wait_ge(s.arrv, n_in)
+        g.remote_dma(out_ap=T.kv[:, r * W + KP:(r + 1) * W], in_ap=T.dv[:], remote_sem=s["fv%d" % r],
+                     local_sem=s.sent, pid=pid, routing_id=rid, dma_engine_mask=m)
+        g.wait_ge(s.sent, 2 * len(_bits(m)))
         return
 
     near = [j for j, d in enumerate(cores) if topo.chip(d) == topo.chip(core)]
@@ -109,48 +113,59 @@ def rank_program(g, core, T, topo):
     peers = [j for j in near if j != rank]
     helpers = [relay_of[(rank, j)] for j in far]
     masks = _split_masks(core, helpers, topo)
+    ko, vo = rank * W, rank * W + KP
 
-    g.sync.dma_start(T.stage[:, 0:KP], T.k[:]).then_inc(s.ld, 16)
-    g.scalar.dma_start(T.stage[:, KP:W], T.v[:]).then_inc(s.ld, 16)
+    g.sync.dma_start(T.dk[:], T.k[:]).then_inc(s.ldk, 16)
+    g.scalar.dma_start(T.dv[:], T.v[:]).then_inc(s.ldv, 16)
     g.sync.dma_start(T.qs[:], T.q[:]).then_inc(s.ldqb, 16)
     g.scalar.dma_start(T.bs[:], T.b[:]).then_inc(s.ldqb, 16)
+    g.sync.dma_start(T.kv[:, ko:ko + KP], T.k[:]).then_inc(s.own, 16)
+    g.scalar.dma_start(T.kv[:, vo:vo + FT], T.v[:]).then_inc(s.own, 16)
     g.vector.memset(T.zero[:], 0.0).then_inc(s.zs, 1)
 
-    g.wait_ge(s.ld, 32)
-    trs = []
-    for h, m in zip(helpers, masks):
-        rid, pid, _se = topo.addr(h)
-        trs.append(RemoteDMATransfer(dst_ids=[DstId(rid=rid, pnc=pid)], dma_engine_mask=m, remote_sem=s.arr,
-                                     src=T.stage[:], dst=T.stage[:]))
-    g.remote_dma_fused(trs, local_sem=s.sent)
-    n_sent = sum(len(_bits(m)) for m in masks)
+    n_sent = 0
+    for ld, buf, arr in ((s.ldk, T.dk, s.arrk), (s.ldv, T.dv, s.arrv)):
+        g.wait_ge(ld, 16)
+        trs = []
+        for h, m in zip(helpers, masks):
+            rid, pid, _se = topo.addr(h)
+            trs.append(RemoteDMATransfer(dst_ids=[DstId(rid=rid, pnc=pid)], dma_engine_mask=m, remote_sem=arr,
+                                         src=buf[:], dst=buf[:]))
+            n_sent += len(_bits(m))
+        g.remote_dma_fused(trs, local_sem=s.sent)
 
-    n_sent2 = 0
+    n_peer_in = 0
     for j in peers:
         rid, pid, _se = topo.addr(cores[j])
-        m = topo.mask(core, cores[j])
-        g.remote_dma(out_ap=T.kv[:, rank * W:(rank + 1) * W], in_ap=T.stage[:], remote_sem=s.peer,
-                     local_sem=s.sent2, pid=pid, routing_id=rid, dma_engine_mask=m)
-        n_sent2 += len(_bits(m))
-
-    g.sync.wait_ge(s.ld, 32)
-    g.sync.wait_ge(s.sent, n_sent)
-    g.sync.dma_start(T.kv[:, rank * W:(rank + 1) * W], T.stage[:]).then_inc(s.own, 16)
+        pm = _split_masks(core, [cores[j], cores[j]], topo)
+        g.remote_dma_fused([
+            RemoteDMATransfer(dst_ids=[DstId(rid=rid, pnc=pid)], dma_engine_mask=pm[0], remote_sem=s.peer,
+                              src=T.dk[:], dst=T.kv[:, ko:ko + KP]),
+            RemoteDMATransfer(dst_ids=[DstId(rid=rid, pnc=pid)], dma_engine_mask=pm[1], remote_sem=s.peer,
+                              src=T.dv[:], dst=T.kv[:, vo:vo + FT]),
+        ], local_sem=s.sent)
+        n_sent += len(_bits(pm[0])) + len(_bits(pm[1]))
+        qm = _split_masks(cores[j], [core, core], topo)
+        n_peer_in += len(_bits(qm[0])) + len(_bits(qm[1]))
 
     g.vector.wait_ge(s.zs, 1)
     g.vector.wait_ge(s.ldqb, 32)
     g.vector.tensor_tensor(out=T.nb[:], in0=T.zero[:], in1=T.bs[:], op=AluOpType.subtract).then_inc(s.nbs, 1)
     g.vector.wait_ge(s.nbs, 1)
 
-    n_peer = sum(len(_bits(topo.mask(cores[j], core))) for j in peers)
-    waits = {rank: [(s.own, 16)]}
+    wk = {rank: (s.own, 32)}
+    wv = {rank: (s.own, 32)}
     for j in peers:
-        waits[j] = [(s.peer, n_peer)]
+        wk[j] = (s.peer, n_peer_in)
+        wv[j] = (s.peer, n_peer_in)
     for j in far:
-        waits[j] = [(s["far%d" % j], len(_bits(topo.mask(relay_of[(j, rank)], core))))]
+        n = len(_bits(topo.mask(relay_of[(j, rank)], core)))
+        wk[j] = (s["fk%d" % j], n)
+        wv[j] = (s["fv%d" % j], n)
     g.tensor.wait_ge(s.ldqb, 32)
-    _group(g, T, [rank] + peers, waits, True, False)
-    _group(g, T, far, waits, False, True)
+    _group(g, T, [rank], wk, wv, True, False)
+    _group(g, T, peers, wk, wv, False, False)
+    _group(g, T, far, wk, wv, False, True)
 
     g.vector.wait_ge(s.mo, 1)
     g.vector.tensor_copy(out=T.ysb[:], in_=T.p_out[:, 0:QP]).then_inc(s.vy, 1)
@@ -159,4 +174,3 @@ def rank_program(g, core, T, topo):
     g.sync.wait_ge(s.st, 16)
 
     g.wait_ge(s.sent, n_sent)
-    g.wait_ge(s.sent2, n_sent2)

from concourse.bass import DstId, RemoteDMATransfer
from concourse.mybir import AluOpType

NSIM = 96
N = 4
QP = 64
KP = 128
FT = 128
W = KP + FT

SCRATCH = {
    "dk": ("dram", [128, KP], "bfloat16"),
    "dv": ("dram", [128, FT], "bfloat16"),
    "kv": ("sbuf", [128, N * W], "bfloat16"),
    "qs": ("sbuf", [128, QP], "bfloat16"),
    "bs": ("sbuf", [128, N * QP], "bfloat16"),
    "nb": ("sbuf", [128, N * QP], "bfloat16"),
    "zero": ("sbuf", [128, N * QP], "bfloat16"),
    "sm": ("sbuf", [128, N * QP], "bfloat16"),
    "ysb": ("sbuf", [128, QP], "bfloat16"),
    "p0": ("psum", [128, 512], "float32"),
    "p1": ("psum", [128, 512], "float32"),
    "p2": ("psum", [128, 512], "float32"),
    "p3": ("psum", [128, 512], "float32"),
    "p_out": ("psum", [128, 512], "float32"),
}
SEMAPHORES = (["ldk", "ldv", "ldqb", "own", "arrk", "arrv", "peer", "sent", "zs", "nbs", "mo", "vy", "st"]
              + ["fk%d" % j for j in range(N)] + ["fv%d" % j for j in range(N)]
              + ["mm%d" % j for j in range(N)] + ["vs%d" % j for j in range(N)])


def _bits(mask):
    return [i for i in range(mask.bit_length()) if (mask >> i) & 1]


def _mask_of(bits):
    m = 0
    for i in bits:
        m |= 1 << i
    return m


def _relays(cores, topo):
    out = {}
    for r, c in enumerate(cores):
        far = [j for j, d in enumerate(cores) if topo.chip(d) != topo.chip(c)]
        helpers = [h for h in range(NSIM)
                   if topo.chip(h) == topo.chip(c) and topo.die(h) == topo.die(c) and h not in cores
                   and all(topo.may_write(h, cores[j]) for j in far)]
        for i, j in enumerate(far):
            out[(r, j)] = helpers[i]
    return out


def _split_masks(core, dsts, topo):
    full = topo.mask(core, dsts[0])
    for h in dsts[1:]:
        full &= topo.mask(core, h)
    bits = _bits(full)
    n = len(bits) // len(dsts)
    return [_mask_of(bits[i * n:(i + 1) * n]) for i in range(len(dsts))]


def _group(g, T, js, wk, wv, first, last):
    s = T.sem
    for j in js:
        g.tensor.wait_ge(wk[j][0], wk[j][1])
        g.tensor.matmul(out=T["p%d" % j][:, 0:QP], lhsT=T.kv[:, j * W:j * W + KP], rhs=T.qs[:],
                        start=True, stop=True).then_inc(s["mm%d" % j], 1)
        g.vector.wait_ge(s["mm%d" % j], 1)
        g.vector.tensor_tensor(out=T.sm[:, j * QP:(j + 1) * QP], in0=T["p%d" % j][:, 0:QP],
                               in1=T.nb[:, j * QP:(j + 1) * QP], op=AluOpType.max).then_inc(s["vs%d" % j], 1)
    for i, j in enumerate(js):
        g.tensor.wait_ge(wv[j][0], wv[j][1])
        g.tensor.matmul(out=T.p_out[:, 0:QP], lhsT=T.kv[:, j * W + KP:(j + 1) * W], rhs=T.bs[:, j * QP:(j + 1) * QP],
                        start=(first and i == 0), stop=False)
    for i, j in enumerate(js):
        g.tensor.wait_ge(s["vs%d" % j], 1)
        end = last and i == len(js) - 1
        ins = g.tensor.matmul(out=T.p_out[:, 0:QP], lhsT=T.kv[:, j * W + KP:(j + 1) * W],
                              rhs=T.sm[:, j * QP:(j + 1) * QP], start=False, stop=end)
        if end:
            ins.then_inc(s.mo, 1)


def rank_program(g, core, T, topo):
    cores = list(T.cores)
    relay_of = _relays(cores, topo)
    s = T.sem
    rank = T.rank_of(core)

    if rank is None:
        jobs = [rj for rj, h in relay_of.items() if h == core]
        if not jobs:
            return
        r, j = jobs[0]
        mine = [relay_of[(r, x)] for x in range(N) if (r, x) in relay_of]
        n_in = len(_bits(_split_masks(cores[r], mine, topo)[mine.index(core)]))
        dst = cores[j]
        rid, pid, _se = topo.addr(dst)
        m = topo.mask(core, dst)
        g.wait_ge(s.arrk, n_in)
        g.remote_dma(out_ap=T.kv[:, r * W:r * W + KP], in_ap=T.dk[:], remote_sem=s["fk%d" % r],
                     local_sem=s.sent, pid=pid, routing_id=rid, dma_engine_mask=m)
        g.wait_ge(s.arrv, n_in)
        g.remote_dma(out_ap=T.kv[:, r * W + KP:(r + 1) * W], in_ap=T.dv[:], remote_sem=s["fv%d" % r],
                     local_sem=s.sent, pid=pid, routing_id=rid, dma_engine_mask=m)
        g.wait_ge(s.sent, 2 * len(_bits(m)))
        return

    near = [j for j, d in enumerate(cores) if topo.chip(d) == topo.chip(core)]
    far = [j for j, d in enumerate(cores) if topo.chip(d) != topo.chip(core)]
    peers = [j for j in near if j != rank]
    helpers = [relay_of[(rank, j)] for j in far]
    masks = _split_masks(core, helpers, topo)
    ko, vo = rank * W, rank * W + KP

    g.sync.dma_start(T.dk[:], T.k[:]).then_inc(s.ldk, 16)
    g.scalar.dma_start(T.dv[:], T.v[:]).then_inc(s.ldv, 16)
    g.sync.dma_start(T.qs[:], T.q[:]).then_inc(s.ldqb, 16)
    g.scalar.dma_start(T.bs[:], T.b[:]).then_inc(s.ldqb, 16)
    g.sync.dma_start(T.kv[:, ko:ko + KP], T.k[:]).then_inc(s.own, 16)
    g.scalar.dma_start(T.kv[:, vo:vo + FT], T.v[:]).then_inc(s.own, 16)
    g.vector.memset(T.zero[:], 0.0).then_inc(s.zs, 1)

    n_sent = 0
    for ld, buf, arr in ((s.ldk, T.dk, s.arrk), (s.ldv, T.dv, s.arrv)):
        g.wait_ge(ld, 16)
        trs = []
        for h, m in zip(helpers, masks):
            rid, pid, _se = topo.addr(h)
            trs.append(RemoteDMATransfer(dst_ids=[DstId(rid=rid, pnc=pid)], dma_engine_mask=m, remote_sem=arr,
                                         src=buf[:], dst=buf[:]))
            n_sent += len(_bits(m))
        g.remote_dma_fused(trs, local_sem=s.sent)

    n_peer_in = 0
    for j in peers:
        rid, pid, _se = topo.addr(cores[j])
        pm = _split_masks(core, [cores[j], cores[j]], topo)
        g.remote_dma_fused([
            RemoteDMATransfer(dst_ids=[DstId(rid=rid, pnc=pid)], dma_engine_mask=pm[0], remote_sem=s.peer,
                              src=T.dk[:], dst=T.kv[:, ko:ko + KP]),
            RemoteDMATransfer(dst_ids=[DstId(rid=rid, pnc=pid)], dma_engine_mask=pm[1], remote_sem=s.peer,
                              src=T.dv[:], dst=T.kv[:, vo:vo + FT]),
        ], local_sem=s.sent)
        n_sent += len(_bits(pm[0])) + len(_bits(pm[1]))
        qm = _split_masks(cores[j], [core, core], topo)
        n_peer_in += len(_bits(qm[0])) + len(_bits(qm[1]))

    g.vector.wait_ge(s.zs, 1)
    g.vector.wait_ge(s.ldqb, 32)
    g.vector.tensor_tensor(out=T.nb[:], in0=T.zero[:], in1=T.bs[:], op=AluOpType.subtract).then_inc(s.nbs, 1)
    g.vector.wait_ge(s.nbs, 1)

    wk = {rank: (s.own, 32)}
    wv = {rank: (s.own, 32)}
    for j in peers:
        wk[j] = (s.peer, n_peer_in)
        wv[j] = (s.peer, n_peer_in)
    for j in far:
        n = len(_bits(topo.mask(relay_of[(j, rank)], core)))
        wk[j] = (s["fk%d" % j], n)
        wv[j] = (s["fv%d" % j], n)
    g.tensor.wait_ge(s.ldqb, 32)
    _group(g, T, [rank], wk, wv, True, False)
    _group(g, T, peers, wk, wv, False, False)
    _group(g, T, far, wk, wv, False, True)

    g.vector.wait_ge(s.mo, 1)
    g.vector.tensor_copy(out=T.ysb[:], in_=T.p_out[:, 0:QP]).then_inc(s.vy, 1)
    g.sync.wait_ge(s.vy, 1)
    g.sync.dma_start(T.y[:], T.ysb[:]).then_inc(s.st, 16)
    g.sync.wait_ge(s.st, 16)

    g.wait_ge(s.sent, n_sent)
